import numpy as np, ml_dtypes
CORES = [2,10,34,50,74,82,98,114,130,138,162,178,202,210,226,242]
N = 16
import mx_ref
NC, D = 512, 4
SRC = [[7,10,11,15],[2,3,12,13],[1,8,9,14],[2,3,6,7],[6,11,12,13],[4,5,9,11],[2,6,9,13],[0,6,9,14],[4,5,8,10],[0,4,14,15],[5,6,14,15],[4,5,7,12],[3,4,10,15],[0,3,11,12],[3,11,13,15],[8,9,10,11]]
BF = ml_dtypes.bfloat16
def setup_inputs(rng):
    def f(*shape):
        return mx_ref.flush((rng.standard_normal(shape, dtype=np.float32) * np.exp2(rng.integers(-2, 3, shape[:-1] + (1,)))).astype(BF))
    return {"w": f(N, 128, D * 512), "x": f(N, 128, 4 * NC)}
def setup_inputs_blocks(rng):
    d = setup_inputs(rng)
    for k in ("w", "x"): d[k] = mx_ref.spread(d[k], rng, 1)
    return d
def setup_inputs_wide(rng):
    d = setup_inputs(rng)
    for k in ("w", "x"): d[k] = mx_ref.flush((d[k].astype(np.float32) * np.exp2(rng.integers(-8, 9, (N, 1, 1))).astype(np.float32)).astype(BF))
    return d
def setup_inputs_zeros(rng):
    d = setup_inputs(rng); v = d["x"].reshape(N, 128, -1, 4).copy()
    v[np.broadcast_to((rng.random((N, 1, v.shape[2], 1)) < 0.33), v.shape)] = 0
    d["x"] = v.reshape(d["x"].shape)
    return d
def reference(w, x):
    QX = [mx_ref.quantize(x[j]) for j in range(N)]
    y = np.zeros((N, 128, NC), np.float32)
    for r in range(N):
        for i in range(D):
            p = mx_ref.matmul(mx_ref.quantize(w[r][:, 512 * i:512 * i + 512]), QX[SRC[r][i]])
            y[r] = p if i == 0 else y[r] + p
    return {"y": y}

@@ -1,0 +1,218 @@
+from concourse.bass import DstId, RemoteDMATransfer
+from concourse.mybir import dt, ActivationFunctionType
+
+WORLD = 256
+NRANKS, NSLICE, COLS = 16, 4, 512
+CUTS = (0, 192, 352, 512)
+NPC = len(CUTS) - 1
+PLANE = NPC
+OUT_LIMIT = 5
+
+SCRATCH = {
+    "xb": ("sbuf", [128, 4 * COLS], "bfloat16"),
+    "wb": ("sbuf", [128, 4 * COLS], "bfloat16"),
+    "qx": ("sbuf", [128, COLS], "float8_e4m3fn_x4"),
+    "sx": ("sbuf", [128, COLS], "uint8"),
+    "qw": ("sbuf", [128, COLS], "float8_e4m3fn_x4"),
+    "sw": ("sbuf", [128, COLS], "uint8"),
+    "ps": ("psum", [128, 512 * NPC], "float32"),
+    "yb": ("sbuf", [128, COLS], "float32"),
+}
+for _i in range(NSLICE):
+    SCRATCH["lc%d" % _i] = ("sbuf", [128, COLS], "float8_e4m3fn_x4")
+    SCRATCH["ls%d" % _i] = ("sbuf", [128, COLS], "uint8")
+
+SEMAPHORES = (["xl%d" % k for k in range(NPC)] + ["xq%d" % k for k in range(NPC)] + ["wl0", "wl1", "wq"]
+              + ["mm%d" % k for k in range(NPC)] + ["cp%d" % k for k in range(NPC)] + ["st", "sent"]
+              + ["a%d_%d" % (j, p) for j in range(NRANKS) for p in range(NPC + 1)])
+
+_PLAN = {}
+
+
+def _bits(m):
+    return bin(m).count("1")
+
+
+def _build(T, topo):
+    cores, src = list(T.cores), T.tables["SRC"]
+    n = len(cores)
+
+    def where(c):
+        return (topo.host(c), topo.chip(c))
+
+    chips = {}
+    for c in range(WORLD):
+        chips.setdefault(where(c), []).append(c)
+    mate_of = {}
+    for a in chips:
+        for b in chips:
+            if topo.mates(chips[a][0], chips[b][0]):
+                mate_of[a] = b
+    rank_at = {where(c): j for j, c in enumerate(cores)}
+    dests = [[r for r in range(n) if j in src[r] and r != j] for j in range(n)]
+
+    colour, busy_s, busy_r = {}, [set() for _ in range(n)], [set() for _ in range(n)]
+    for j in sorted(range(n), key=lambda q: -len(dests[q])):
+        for r in sorted(dests[j], key=lambda q: (q - j) % n):
+            k = 0
+            while k in busy_s[j] or k in busy_r[r]:
+                k += 1
+            colour[(j, r)] = k
+            busy_s[j].add(k)
+            busy_r[r].add(k)
+    for j in range(n):
+        dests[j].sort(key=lambda r: colour[(j, r)])
+
+    near = [[r for r in dests[j] if topo.same_plane(cores[j], cores[r])] for j in range(n)]
+    far = [[r for r in dests[j] if r not in near[j]] for j in range(n)]
+
+    tasks, taken, away = {}, set(cores), set()
+    idle_used = set()
+    for j in range(n):
+        me, home = cores[j], where(cores[j])
+        groups = [(home, dests[j])]
+        neighbour = rank_at.get(mate_of[home])
+        crowd = len(far[j]) + (len(near[neighbour]) if neighbour is not None else 0)
+        if far[j] and crowd > OUT_LIMIT:
+            idle = [k for k in chips if k not in rank_at and mate_of[k] not in rank_at and k not in idle_used
+                    and all(topo.same_plane(chips[k][0], cores[r]) for r in far[j])]
+            if idle:
+                idle_used.add(idle[0])
+                away.add(j)
+                groups = ([(home, near[j])] if near[j] else []) + [(idle[0], far[j])]
+        stage = [[] for _ in range(NPC + 1)]
+        own_plane = []
+        for place, dl in groups:
+            ok = [c for c in chips[place] if c not in taken and topo.may_write(me, c)
+                  and all(topo.may_write(c, cores[r]) for r in dl)]
+            same = [c for c in ok if topo.die(c) == topo.die(me)]
+            other = [c for c in ok if topo.die(c) != topo.die(me)]
+            senders = [same[0], other[0], other[1]]
+            if place != home:
+                senders.append(same[1])
+            else:
+                own_plane = dl
+            taken.update(senders)
+            for p, c in enumerate(senders):
+                stage[p].append(c)
+                tasks[c] = [(j, p, [(cores[r], src[r].index(j)) for r in dl])]
+        mine = [(j, p, [(c, -1) for c in stage[p]]) for p in range(NPC)]
+        if stage[PLANE]:
+            mine.append((j, PLANE, [(c, -1) for c in stage[PLANE]]))
+        if own_plane:
+            mine.append((j, PLANE, [(cores[r], src[r].index(j)) for r in own_plane]))
+        tasks[me] = mine
+
+    mask, sender = {}, {}
+    for c, calls in tasks.items():
+        m = -1
+        for j, p, targets in calls:
+            for d, _slot in targets:
+                m &= topo.mask(c, d)
+                sender[(j, p, d)] = c
+        mask[c] = m
+    order = []
+    for r in range(n):
+        def key(i, r=r):
+            j = src[r][i]
+            return -1 if j == r else colour[(j, r)] + (1 if j in away else 0)
+        order.append(sorted(range(len(src[r])), key=key))
+    return {"tasks": tasks, "mask": mask, "sender": sender, "order": order}
+
+
+def _piece(T, codes, plane, p):
+    if p == PLANE:
+        return T[plane][:, 0:COLS]
+    return T[codes][:, CUTS[p]:CUTS[p + 1]].bitcast(dt.uint8)
+
+
+def _send(g, core, T, topo, plan, call):
+    j, p, targets = call
+    ids, dsts = [], []
+    for d, slot in targets:
+        rid, pid = topo.addr(d, core)
+        ids.append(DstId(rid=rid, pnc=pid))
+        dsts.append(_piece(T, "qx", "sx", p) if slot < 0 else _piece(T, "lc%d" % slot, "ls%d" % slot, p))
+    m = plan["mask"][core]
+    g.remote_dma_fused([RemoteDMATransfer(dst_ids=ids, dma_engine_mask=m, remote_sem=T.sem["a%d_%d" % (j, p)],
+                                          srcs=[_piece(T, "qx", "sx", p)], dsts=dsts)], local_sem=T.sem.sent)
+    return _bits(m)
+
+
+def rank_program(g, core, T, topo):
+    if "plan" not in _PLAN:
+        _PLAN["plan"] = _build(T, topo)
+    plan = _PLAN["plan"]
+    calls = plan["tasks"].get(core)
+    if calls is None:
+        return
+    rank = T.rank_of(core)
+    sem = T.sem
+
+    if rank is None:
+        left = 0
+        for call in calls:
+            j, p, _targets = call
+            g.wait_ge(sem["a%d_%d" % (j, p)], _bits(plan["mask"][plan["sender"][(j, p, core)]]))
+            left += _send(g, core, T, topo, plan, call)
+        g.wait_ge(sem.sent, left)
+        return
+
+    src = T.tables["SRC"][rank]
+    queues = [g.sync, g.scalar]
+    for k in range(NPC):
+        a, b = 4 * CUTS[k], 4 * CUTS[k + 1]
+        queues[k % 2].dma_start(T.xb[:, a:b], T.x[:, a:b]).then_inc(sem["xl%d" % k], 16)
+    half = 2 * COLS
+    for h in range(2):
+        queues[(NPC + h) % 2].dma_start(T.wb[:, h * half:(h + 1) * half],
+                                        T.w[:, h * half:(h + 1) * half]).then_inc(sem["wl%d" % h], 16)
+
+    for k in range(NPC):
+        a, b = CUTS[k], CUTS[k + 1]
+        g.vector.wait_ge(sem["xl%d" % k], 16)
+        g.vector.quantize_mx(T.qx[:, a:b], T.sx[:, a:b], T.xb[:, 4 * a:4 * b]).then_inc(sem["xq%d" % k], 1)
+    for h in range(2):
+        a, b = h * COLS // 2, (h + 1) * COLS // 2
+        g.vector.wait_ge(sem["wl%d" % h], 16)
+        g.vector.quantize_mx(T.qw[:, a:b], T.sw[:, a:b], T.wb[:, 4 * a:4 * b]).then_inc(sem.wq, 1)
+
+    left = 0
+    for call in calls:
+        if call[1] < NPC:
+            g.wait_ge(sem["xq%d" % call[1]], 1)
+        left += _send(g, core, T, topo, plan, call)
+
+    g.tensor.wait_ge(sem.wq, 2)
+    order = plan["order"][rank]
+    for pos, i in enumerate(order):
+        j = src[i]
+        own = j == rank
+        codes, plane = ("qx", "sx") if own else ("lc%d" % i, "ls%d" % i)
+        if not own:
+            g.tensor.wait_ge(sem["a%d_%d" % (j, PLANE)], _bits(plan["mask"][plan["sender"][(j, PLANE, core)]]))
+        for k in range(NPC):
+            a, b = CUTS[k], CUTS[k + 1]
+            if own:
+                g.tensor.wait_ge(sem["xq%d" % k], 1)
+            else:
+                g.tensor.wait_ge(sem["a%d_%d" % (j, k)], _bits(plan["mask"][plan["sender"][(j, k, core)]]))
+            mm = g.tensor.matmul_mx(T.ps[:, 512 * k:512 * k + (b - a)], T.qw[:, 128 * i:128 * i + 128],
+                                    T.sw[:, 128 * i:128 * i + 128], T[codes][:, a:b], T[plane][:, a:b],
+                                    pos == 0, pos == len(order) - 1)
+            if pos == len(order) - 1:
+                mm.then_inc(sem["mm%d" % k], 1)
+
+    for k in range(NPC):
+        a, b = CUTS[k], CUTS[k + 1]
+        bank = T.ps[:, 512 * k:512 * k + (b - a)]
+        if k % 2 == 0:
+            g.vector.wait_ge(sem["mm%d" % k], 1)
+            g.vector.tensor_copy(T.yb[:, a:b], bank).then_inc(sem["cp%d" % k], 1)
+        else:
+            g.scalar.wait_ge(sem["mm%d" % k], 1)
+            g.scalar.activation(T.yb[:, a:b], bank, ActivationFunctionType.Copy).then_inc(sem["cp%d" % k], 1)
+        queues[k % 2].wait_ge(sem["cp%d" % k], 1)
+        queues[k % 2].dma_start(T.y[:, a:b], T.yb[:, a:b]).then_inc(sem.st, 16)
+    g.sync.wait_ge(sem.st, 16 * NPC)
+    g.wait_ge(sem.sent, left)

@@ -3,10 +3,11 @@ from concourse.mybir import dt, ActivationFunctionType
 
 WORLD = 256
 NRANKS, NSLICE, COLS = 16, 4, 512
-CUTS = (0, 192, 352, 512)
+CUTS = (0, 128, 352, 512)
 NPC = len(CUTS) - 1
 PLANE = NPC
 OUT_LIMIT = 5
+SPLIT = 4
 
 SCRATCH = {
     "xb": ("sbuf", [128, 4 * COLS], "bfloat16"),
@@ -49,75 +50,98 @@ def _build(T, topo):
             if topo.mates(chips[a][0], chips[b][0]):
                 mate_of[a] = b
     rank_at = {where(c): j for j, c in enumerate(cores)}
-    dests = [[r for r in range(n) if j in src[r] and r != j] for j in range(n)]
-
-    colour, busy_s, busy_r = {}, [set() for _ in range(n)], [set() for _ in range(n)]
-    for j in sorted(range(n), key=lambda q: -len(dests[q])):
-        for r in sorted(dests[j], key=lambda q: (q - j) % n):
-            k = 0
-            while k in busy_s[j] or k in busy_r[r]:
-                k += 1
-            colour[(j, r)] = k
-            busy_s[j].add(k)
-            busy_r[r].add(k)
-    for j in range(n):
-        dests[j].sort(key=lambda r: colour[(j, r)])
-
+    dests = [sorted([r for r in range(n) if j in src[r] and r != j], key=lambda q, j=j: (q - j) % n) for j in range(n)]
     near = [[r for r in dests[j] if topo.same_plane(cores[j], cores[r])] for j in range(n)]
     far = [[r for r in dests[j] if r not in near[j]] for j in range(n)]
 
-    tasks, taken, away = {}, set(cores), set()
-    idle_used = set()
+    groups, idle_used = [], set()
     for j in range(n):
-        me, home = cores[j], where(cores[j])
-        groups = [(home, dests[j])]
+        home = where(cores[j])
         neighbour = rank_at.get(mate_of[home])
-        crowd = len(far[j]) + (len(near[neighbour]) if neighbour is not None else 0)
-        if far[j] and crowd > OUT_LIMIT:
+        theirs = len(near[neighbour]) if neighbour is not None else 0
+        gl = None
+        if far[j] and len(far[j]) + theirs > OUT_LIMIT:
             idle = [k for k in chips if k not in rank_at and mate_of[k] not in rank_at and k not in idle_used
                     and all(topo.same_plane(chips[k][0], cores[r]) for r in far[j])]
             if idle:
                 idle_used.add(idle[0])
-                away.add(j)
-                groups = ([(home, near[j])] if near[j] else []) + [(idle[0], far[j])]
+                room = max(0, OUT_LIMIT - theirs - 1)
+                stay = far[j][:room] + near[j]
+                gl = [(idle[0], far[j][room:])] + ([(home, stay)] if stay else [])
+        if gl is None:
+            k = len(dests[j])
+            if k >= SPLIT and near[j]:
+                first = max(len(far[j]), (k + 1) // 2)
+                both = far[j] + near[j]
+                gl = [(home, both[:first])] + ([(home, both[first:])] if both[first:] else [])
+            else:
+                gl = [(home, far[j] + near[j])]
+        groups.append(gl)
+
+    colour, busy_r = {}, [set() for _ in range(n)]
+    sets = [(j, gi) for j in range(n) for gi in range(len(groups[j]))]
+    for j, gi in sorted(sets, key=lambda s: -len(groups[s[0]][s[1]][1])):
+        used = set()
+        for r in sorted(groups[j][gi][1], key=lambda q, j=j: (q - j) % n):
+            k = 0
+            while k in used or k in busy_r[r]:
+                k += 1
+            colour[(j, r)] = k
+            used.add(k)
+            busy_r[r].add(k)
+        groups[j][gi][1].sort(key=lambda r, j=j: colour[(j, r)])
+
+    tasks, taken, late = {}, set(cores), set()
+    for j in range(n):
+        me, home = cores[j], where(cores[j])
         stage = [[] for _ in range(NPC + 1)]
         own_plane = []
-        for place, dl in groups:
+        for place, dl in groups[j]:
             ok = [c for c in chips[place] if c not in taken and topo.may_write(me, c)
                   and all(topo.may_write(c, cores[r]) for r in dl)]
             same = [c for c in ok if topo.die(c) == topo.die(me)]
             other = [c for c in ok if topo.die(c) != topo.die(me)]
-            senders = [same[0], other[0], other[1]]
+            senders = [other[0], same[0], other[1]]
             if place != home:
                 senders.append(same[1])
+                late.update((j, r) for r in dl)
             else:
-                own_plane = dl
+                own_plane += dl
             taken.update(senders)
             for p, c in enumerate(senders):
                 stage[p].append(c)
-                tasks[c] = [(j, p, [(cores[r], src[r].index(j)) for r in dl])]
-        mine = [(j, p, [(c, -1) for c in stage[p]]) for p in range(NPC)]
-        if stage[PLANE]:
-            mine.append((j, PLANE, [(c, -1) for c in stage[PLANE]]))
+                m = -1
+                for r in dl:
+                    m &= topo.mask(c, cores[r])
+                tasks[c] = [[(j, p, m, [(cores[r], src[r].index(j)) for r in dl])]]
+        own_plane.sort(key=lambda r, j=j: colour[(j, r)])
+        low, full = -1, 0
+        for c in [c for p in stage for c in p] + [cores[r] for r in own_plane]:
+            low &= topo.mask(me, c)
+            full |= topo.mask(me, c)
+        high = full & ~low
+        mine = []
+        for p in range(NPC + 1):
+            if stage[p]:
+                masks = [low] + [high] * (len(stage[p]) - 1)
+                mine.append([(j, p, masks[q], [(c, -1)]) for q, c in enumerate(stage[p])])
         if own_plane:
-            mine.append((j, PLANE, [(cores[r], src[r].index(j)) for r in own_plane]))
+            mine.append([(j, PLANE, low, [(cores[r], src[r].index(j)) for r in own_plane])])
         tasks[me] = mine
 
-    mask, sender = {}, {}
+    arrive = {}
     for c, calls in tasks.items():
-        m = -1
-        for j, p, targets in calls:
-            for d, _slot in targets:
-                m &= topo.mask(c, d)
-                sender[(j, p, d)] = c
-        mask[c] = m
+        for call in calls:
+            for j, p, m, targets in call:
+                for d, _slot in targets:
+                    arrive[(j, p, d)] = _bits(m)
     order = []
     for r in range(n):
         def key(i, r=r):
             j = src[r][i]
-            return -1 if j == r else colour[(j, r)] + (1 if j in away else 0)
+            return -1 if j == r else colour[(j, r)] + (1 if (j, r) in late else 0)
         order.append(sorted(range(len(src[r])), key=key))
-    return {"tasks": tasks, "mask": mask, "sender": sender, "order": order}
+    return {"tasks": tasks, "arrive": arrive, "order": order}
 
 
 def _piece(T, codes, plane, p):
@@ -126,17 +150,19 @@ def _piece(T, codes, plane, p):
     return T[codes][:, CUTS[p]:CUTS[p + 1]].bitcast(dt.uint8)
 
 
-def _send(g, core, T, topo, plan, call):
-    j, p, targets = call
-    ids, dsts = [], []
-    for d, slot in targets:
-        rid, pid = topo.addr(d, core)
-        ids.append(DstId(rid=rid, pnc=pid))
-        dsts.append(_piece(T, "qx", "sx", p) if slot < 0 else _piece(T, "lc%d" % slot, "ls%d" % slot, p))
-    m = plan["mask"][core]
-    g.remote_dma_fused([RemoteDMATransfer(dst_ids=ids, dma_engine_mask=m, remote_sem=T.sem["a%d_%d" % (j, p)],
-                                          srcs=[_piece(T, "qx", "sx", p)], dsts=dsts)], local_sem=T.sem.sent)
-    return _bits(m)
+def _send(g, core, T, topo, call):
+    transfers, left = [], 0
+    for j, p, m, targets in call:
+        ids, dsts = [], []
+        for d, slot in targets:
+            rid, pid = topo.addr(d, core)
+            ids.append(DstId(rid=rid, pnc=pid))
+            dsts.append(_piece(T, "qx", "sx", p) if slot < 0 else _piece(T, "lc%d" % slot, "ls%d" % slot, p))
+        transfers.append(RemoteDMATransfer(dst_ids=ids, dma_engine_mask=m, remote_sem=T.sem["a%d_%d" % (j, p)],
+                                           srcs=[_piece(T, "qx", "sx", p)], dsts=dsts))
+        left += _bits(m)
+    g.remote_dma_fused(transfers, local_sem=T.sem.sent)
+    return left
 
 
 def rank_program(g, core, T, topo):
@@ -148,29 +174,34 @@ def rank_program(g, core, T, topo):
         return
     rank = T.rank_of(core)
     sem = T.sem
+    arrive = plan["arrive"]
 
     if rank is None:
         left = 0
         for call in calls:
-            j, p, _targets = call
-            g.wait_ge(sem["a%d_%d" % (j, p)], _bits(plan["mask"][plan["sender"][(j, p, core)]]))
-            left += _send(g, core, T, topo, plan, call)
+            j, p = call[0][0], call[0][1]
+            g.wait_ge(sem["a%d_%d" % (j, p)], arrive[(j, p, core)])
+            left += _send(g, core, T, topo, call)
         g.wait_ge(sem.sent, left)
         return
 
     src = T.tables["SRC"][rank]
     queues = [g.sync, g.scalar]
-    for k in range(NPC):
+    rows = T.xb.shape[0] // 2
+    for h in range(2):
+        queues[h].dma_start(T.xb[h * rows:(h + 1) * rows, 0:4 * CUTS[1]],
+                            T.x[h * rows:(h + 1) * rows, 0:4 * CUTS[1]]).then_inc(sem.xl0, 16)
+    for k in range(1, NPC):
         a, b = 4 * CUTS[k], 4 * CUTS[k + 1]
-        queues[k % 2].dma_start(T.xb[:, a:b], T.x[:, a:b]).then_inc(sem["xl%d" % k], 16)
+        queues[(k - 1) % 2].dma_start(T.xb[:, a:b], T.x[:, a:b]).then_inc(sem["xl%d" % k], 16)
     half = 2 * COLS
     for h in range(2):
-        queues[(NPC + h) % 2].dma_start(T.wb[:, h * half:(h + 1) * half],
-                                        T.w[:, h * half:(h + 1) * half]).then_inc(sem["wl%d" % h], 16)
+        queues[h].dma_start(T.wb[:, h * half:(h + 1) * half],
+                            T.w[:, h * half:(h + 1) * half]).then_inc(sem["wl%d" % h], 16)
 
     for k in range(NPC):
         a, b = CUTS[k], CUTS[k + 1]
-        g.vector.wait_ge(sem["xl%d" % k], 16)
+        g.vector.wait_ge(sem["xl%d" % k], 32 if k == 0 else 16)
         g.vector.quantize_mx(T.qx[:, a:b], T.sx[:, a:b], T.xb[:, 4 * a:4 * b]).then_inc(sem["xq%d" % k], 1)
     for h in range(2):
         a, b = h * COLS // 2, (h + 1) * COLS // 2
@@ -179,9 +210,9 @@ def rank_program(g, core, T, topo):
 
     left = 0
     for call in calls:
-        if call[1] < NPC:
-            g.wait_ge(sem["xq%d" % call[1]], 1)
-        left += _send(g, core, T, topo, plan, call)
+        if call[0][1] < NPC:
+            g.wait_ge(sem["xq%d" % call[0][1]], 1)
+        left += _send(g, core, T, topo, call)
 
     g.tensor.wait_ge(sem.wq, 2)
     order = plan["order"][rank]
@@ -190,13 +221,13 @@ def rank_program(g, core, T, topo):
         own = j == rank
         codes, plane = ("qx", "sx") if own else ("lc%d" % i, "ls%d" % i)
         if not own:
-            g.tensor.wait_ge(sem["a%d_%d" % (j, PLANE)], _bits(plan["mask"][plan["sender"][(j, PLANE, core)]]))
+            g.tensor.wait_ge(sem["a%d_%d" % (j, PLANE)], arrive[(j, PLANE, core)])
         for k in range(NPC):
             a, b = CUTS[k], CUTS[k + 1]
             if own:
                 g.tensor.wait_ge(sem["xq%d" % k], 1)
             else:
-                g.tensor.wait_ge(sem["a%d_%d" % (j, k)], _bits(plan["mask"][plan["sender"][(j, k, core)]]))
+                g.tensor.wait_ge(sem["a%d_%d" % (j, k)], arrive[(j, k, core)])
             mm = g.tensor.matmul_mx(T.ps[:, 512 * k:512 * k + (b - a)], T.qw[:, 128 * i:128 * i + 128],
                                     T.sw[:, 128 * i:128 * i + 128], T[codes][:, a:b], T[plane][:, a:b],
                                     pos == 0, pos == len(order) - 1)

from concourse.bass import DstId, RemoteDMATransfer
from concourse.mybir import dt, ActivationFunctionType

WORLD = 256
NRANKS, NSLICE, COLS = 16, 4, 512
CUTS = (0, 128, 352, 512)
NPC = len(CUTS) - 1
PLANE = NPC
OUT_LIMIT = 5
SPLIT = 4

SCRATCH = {
    "xb": ("sbuf", [128, 4 * COLS], "bfloat16"),
    "wb": ("sbuf", [128, 4 * COLS], "bfloat16"),
    "qx": ("sbuf", [128, COLS], "float8_e4m3fn_x4"),
    "sx": ("sbuf", [128, COLS], "uint8"),
    "qw": ("sbuf", [128, COLS], "float8_e4m3fn_x4"),
    "sw": ("sbuf", [128, COLS], "uint8"),
    "ps": ("psum", [128, 512 * NPC], "float32"),
    "yb": ("sbuf", [128, COLS], "float32"),
}
for _i in range(NSLICE):
    SCRATCH["lc%d" % _i] = ("sbuf", [128, COLS], "float8_e4m3fn_x4")
    SCRATCH["ls%d" % _i] = ("sbuf", [128, COLS], "uint8")

SEMAPHORES = (["xl%d" % k for k in range(NPC)] + ["xq%d" % k for k in range(NPC)] + ["wl0", "wl1", "wq"]
              + ["mm%d" % k for k in range(NPC)] + ["cp%d" % k for k in range(NPC)] + ["st", "sent"]
              + ["a%d_%d" % (j, p) for j in range(NRANKS) for p in range(NPC + 1)])

_PLAN = {}


def _bits(m):
    return bin(m).count("1")


def _build(T, topo):
    cores, src = list(T.cores), T.tables["SRC"]
    n = len(cores)

    def where(c):
        return (topo.host(c), topo.chip(c))

    chips = {}
    for c in range(WORLD):
        chips.setdefault(where(c), []).append(c)
    mate_of = {}
    for a in chips:
        for b in chips:
            if topo.mates(chips[a][0], chips[b][0]):
                mate_of[a] = b
    rank_at = {where(c): j for j, c in enumerate(cores)}
    dests = [sorted([r for r in range(n) if j in src[r] and r != j], key=lambda q, j=j: (q - j) % n) for j in range(n)]
    near = [[r for r in dests[j] if topo.same_plane(cores[j], cores[r])] for j in range(n)]
    far = [[r for r in dests[j] if r not in near[j]] for j in range(n)]

    groups, idle_used = [], set()
    for j in range(n):
        home = where(cores[j])
        neighbour = rank_at.get(mate_of[home])
        theirs = len(near[neighbour]) if neighbour is not None else 0
        gl = None
        if far[j] and len(far[j]) + theirs > OUT_LIMIT:
            idle = [k for k in chips if k not in rank_at and mate_of[k] not in rank_at and k not in idle_used
                    and all(topo.same_plane(chips[k][0], cores[r]) for r in far[j])]
            if idle:
                idle_used.add(idle[0])
                room = max(0, OUT_LIMIT - theirs - 1)
                stay = far[j][:room] + near[j]
                gl = [(idle[0], far[j][room:])] + ([(home, stay)] if stay else [])
        if gl is None:
            k = len(dests[j])
            if k >= SPLIT and near[j]:
                first = max(len(far[j]), (k + 1) // 2)
                both = far[j] + near[j]
                gl = [(home, both[:first])] + ([(home, both[first:])] if both[first:] else [])
            else:
                gl = [(home, far[j] + near[j])]
        groups.append(gl)

    colour, busy_r = {}, [set() for _ in range(n)]
    sets = [(j, gi) for j in range(n) for gi in range(len(groups[j]))]
    for j, gi in sorted(sets, key=lambda s: -len(groups[s[0]][s[1]][1])):
        used = set()
        for r in sorted(groups[j][gi][1], key=lambda q, j=j: (q - j) % n):
            k = 0
            while k in used or k in busy_r[r]:
                k += 1
            colour[(j, r)] = k
            used.add(k)
            busy_r[r].add(k)
        groups[j][gi][1].sort(key=lambda r, j=j: colour[(j, r)])

    tasks, taken, late = {}, set(cores), set()
    for j in range(n):
        me, home = cores[j], where(cores[j])
        stage = [[] for _ in range(NPC + 1)]
        own_plane = []
        for place, dl in groups[j]:
            ok = [c for c in chips[place] if c not in taken and topo.may_write(me, c)
                  and all(topo.may_write(c, cores[r]) for r in dl)]
            same = [c for c in ok if topo.die(c) == topo.die(me)]
            other = [c for c in ok if topo.die(c) != topo.die(me)]
            senders = [other[0], same[0], other[1]]
            if place != home:
                senders.append(same[1])
                late.update((j, r) for r in dl)
            else:
                own_plane += dl
            taken.update(senders)
            for p, c in enumerate(senders):
                stage[p].append(c)
                m = -1
                for r in dl:
                    m &= topo.mask(c, cores[r])
                tasks[c] = [[(j, p, m, [(cores[r], src[r].index(j)) for r in dl])]]
        own_plane.sort(key=lambda r, j=j: colour[(j, r)])
        low, full = -1, 0
        for c in [c for p in stage for c in p] + [cores[r] for r in own_plane]:
            low &= topo.mask(me, c)
            full |= topo.mask(me, c)
        high = full & ~low
        mine = []
        for p in range(NPC + 1):
            if stage[p]:
                masks = [low] + [high] * (len(stage[p]) - 1)
                mine.append([(j, p, masks[q], [(c, -1)]) for q, c in enumerate(stage[p])])
        if own_plane:
            mine.append([(j, PLANE, low, [(cores[r], src[r].index(j)) for r in own_plane])])
        tasks[me] = mine

    arrive = {}
    for c, calls in tasks.items():
        for call in calls:
            for j, p, m, targets in call:
                for d, _slot in targets:
                    arrive[(j, p, d)] = _bits(m)
    order = []
    for r in range(n):
        def key(i, r=r):
            j = src[r][i]
            return -1 if j == r else colour[(j, r)] + (1 if (j, r) in late else 0)
        order.append(sorted(range(len(src[r])), key=key))
    return {"tasks": tasks, "arrive": arrive, "order": order}


def _piece(T, codes, plane, p):
    if p == PLANE:
        return T[plane][:, 0:COLS]
    return T[codes][:, CUTS[p]:CUTS[p + 1]].bitcast(dt.uint8)


def _send(g, core, T, topo, call):
    transfers, left = [], 0
    for j, p, m, targets in call:
        ids, dsts = [], []
        for d, slot in targets:
            rid, pid = topo.addr(d, core)
            ids.append(DstId(rid=rid, pnc=pid))
            dsts.append(_piece(T, "qx", "sx", p) if slot < 0 else _piece(T, "lc%d" % slot, "ls%d" % slot, p))
        transfers.append(RemoteDMATransfer(dst_ids=ids, dma_engine_mask=m, remote_sem=T.sem["a%d_%d" % (j, p)],
                                           srcs=[_piece(T, "qx", "sx", p)], dsts=dsts))
        left += _bits(m)
    g.remote_dma_fused(transfers, local_sem=T.sem.sent)
    return left


def rank_program(g, core, T, topo):
    if "plan" not in _PLAN:
        _PLAN["plan"] = _build(T, topo)
    plan = _PLAN["plan"]
    calls = plan["tasks"].get(core)
    if calls is None:
        return
    rank = T.rank_of(core)
    sem = T.sem
    arrive = plan["arrive"]

    if rank is None:
        left = 0
        for call in calls:
            j, p = call[0][0], call[0][1]
            g.wait_ge(sem["a%d_%d" % (j, p)], arrive[(j, p, core)])
            left += _send(g, core, T, topo, call)
        g.wait_ge(sem.sent, left)
        return

    src = T.tables["SRC"][rank]
    queues = [g.sync, g.scalar]
    rows = T.xb.shape[0] // 2
    for h in range(2):
        queues[h].dma_start(T.xb[h * rows:(h + 1) * rows, 0:4 * CUTS[1]],
                            T.x[h * rows:(h + 1) * rows, 0:4 * CUTS[1]]).then_inc(sem.xl0, 16)
    for k in range(1, NPC):
        a, b = 4 * CUTS[k], 4 * CUTS[k + 1]
        queues[(k - 1) % 2].dma_start(T.xb[:, a:b], T.x[:, a:b]).then_inc(sem["xl%d" % k], 16)
    half = 2 * COLS
    for h in range(2):
        queues[h].dma_start(T.wb[:, h * half:(h + 1) * half],
                            T.w[:, h * half:(h + 1) * half]).then_inc(sem["wl%d" % h], 16)

    for k in range(NPC):
        a, b = CUTS[k], CUTS[k + 1]
        g.vector.wait_ge(sem["xl%d" % k], 32 if k == 0 else 16)
        g.vector.quantize_mx(T.qx[:, a:b], T.sx[:, a:b], T.xb[:, 4 * a:4 * b]).then_inc(sem["xq%d" % k], 1)
    for h in range(2):
        a, b = h * COLS // 2, (h + 1) * COLS // 2
        g.vector.wait_ge(sem["wl%d" % h], 16)
        g.vector.quantize_mx(T.qw[:, a:b], T.sw[:, a:b], T.wb[:, 4 * a:4 * b]).then_inc(sem.wq, 1)

    left = 0
    for call in calls:
        if call[0][1] < NPC:
            g.wait_ge(sem["xq%d" % call[0][1]], 1)
        left += _send(g, core, T, topo, call)

    g.tensor.wait_ge(sem.wq, 2)
    order = plan["order"][rank]
    for pos, i in enumerate(order):
        j = src[i]
        own = j == rank
        codes, plane = ("qx", "sx") if own else ("lc%d" % i, "ls%d" % i)
        if not own:
            g.tensor.wait_ge(sem["a%d_%d" % (j, PLANE)], arrive[(j, PLANE, core)])
        for k in range(NPC):
            a, b = CUTS[k], CUTS[k + 1]
            if own:
                g.tensor.wait_ge(sem["xq%d" % k], 1)
            else:
                g.tensor.wait_ge(sem["a%d_%d" % (j, k)], arrive[(j, k, core)])
            mm = g.tensor.matmul_mx(T.ps[:, 512 * k:512 * k + (b - a)], T.qw[:, 128 * i:128 * i + 128],
                                    T.sw[:, 128 * i:128 * i + 128], T[codes][:, a:b], T[plane][:, a:b],
                                    pos == 0, pos == len(order) - 1)
            if pos == len(order) - 1:
                mm.then_inc(sem["mm%d" % k], 1)

    for k in range(NPC):
        a, b = CUTS[k], CUTS[k + 1]
        bank = T.ps[:, 512 * k:512 * k + (b - a)]
        if k % 2 == 0:
            g.vector.wait_ge(sem["mm%d" % k], 1)
            g.vector.tensor_copy(T.yb[:, a:b], bank).then_inc(sem["cp%d" % k], 1)
        else:
            g.scalar.wait_ge(sem["mm%d" % k], 1)
            g.scalar.activation(T.yb[:, a:b], bank, ActivationFunctionType.Copy).then_inc(sem["cp%d" % k], 1)
        queues[k % 2].wait_ge(sem["cp%d" % k], 1)
        queues[k % 2].dma_start(T.y[:, a:b], T.yb[:, a:b]).then_inc(sem.st, 16)
    g.sync.wait_ge(sem.st, 16 * NPC)
    g.wait_ge(sem.sent, left)
